import numpy as np
import ml_dtypes


def mxq(x, axis, fmt="e4m3"):
    dtype, down = {"e4m3": (ml_dtypes.float8_e4m3fn, 7), "e5m2": (ml_dtypes.float8_e5m2, 14)}[fmt]
    v = np.moveaxis(np.asarray(x, np.float32).astype(ml_dtypes.bfloat16).astype(np.float64), axis, -1)
    blocks = v.reshape(v.shape[:-1] + (-1, 32))
    amax = np.abs(blocks).max(-1, keepdims=True)
    byte = np.maximum(np.where(amax > 0, np.frexp(amax)[1] - 1 + 127, 0) - down, 1)
    scale = np.exp2(byte - 127.0)
    codes = (blocks / scale).astype(np.float32).astype(dtype).astype(np.float64)
    return np.moveaxis((codes * scale).reshape(v.shape), -1, axis)


WIDE = False


def mx_kscale(k):
    if not WIDE:
        return np.ones(k)
    levels = np.array([10, -10, 5, -5, 0])
    if k % 512:
        return np.exp2(np.random.permutation(np.resize(levels, k // 32))).repeat(32)
    a = np.empty((k // 512, 16))
    for p in range(k // 512):
        a[p, :8] = np.random.permutation(np.resize(levels, 8))
        for g in range(8):
            far = levels[np.abs(levels - a[p, g]) >= 10]
            a[p, g + 8] = far[np.random.randint(len(far))]
    return np.exp2(a.ravel()).repeat(32)


def f64(x):
    return np.asarray(x).astype(np.float64)


def striped(idx):
    return np.tile(idx.reshape(-1, 16).T, (8, 1)).astype(np.uint16)


def unstriped(offs):
    return offs[:16].T.reshape(-1).astype(np.int64)


def striped8(idx):
    return np.concatenate([x.reshape(-1, 16).T for x in idx]).astype(np.uint16)


def runs(offs, k):
    lists = np.stack([offs[16 * r : 16 * r + 16].T.reshape(-1) for r in range(8)]).astype(np.int64)
    return lists[np.arange(k) % 512 // 64]


def pack_weight(w):
    k, n = w.shape
    w = f64(np.asarray(w, np.float32).astype(ml_dtypes.bfloat16)).reshape(k // 32, 32, n)
    amax = np.abs(w).max(1)
    byte = np.clip(np.where(amax > 0, np.frexp(amax)[1] - 1 + 127 - 7, 1), 1, 254)
    scaled = (w * np.exp2(127.0 - byte)[:, None, :]).reshape(k, n).astype(np.float32)
    words = np.ascontiguousarray(scaled.reshape(k // 512, 128, 4, n).transpose(0, 1, 3, 2)).astype(ml_dtypes.float8_e4m3fn).view(np.uint8)
    return words, np.ascontiguousarray(byte.astype(np.uint8).reshape(k // 512, 16, n))


def unpack_weight(words, scales):
    g, p, n, _ = words.shape
    vals = np.ascontiguousarray(words).view(ml_dtypes.float8_e4m3fn).astype(np.float64) * np.repeat(np.exp2(scales.astype(np.float64) - 127.0), 8, axis=1)[..., None]
    return vals.transpose(0, 1, 3, 2).reshape(g * 512, n)


E2M1 = np.array([0.0, 0.5, 1.0, 1.5, 2.0, 3.0, 4.0, 6.0, -0.0, -0.5, -1.0, -1.5, -2.0, -3.0, -4.0, -6.0])


def pack_fp4(w):
    k, n = w.shape
    w = f64(np.asarray(w, np.float32).astype(ml_dtypes.bfloat16)).reshape(k // 32, 32, n)
    amax = np.abs(w).max(1)
    mant, ex = np.frexp(amax / 6.0)
    byte = np.clip(np.where(amax > 0, np.where(mant > 0.5, ex, ex - 1) + 127, 1), 1, 254)
    scaled = (w * np.exp2(127.0 - byte)[:, None, :]).reshape(k, n).astype(np.float32)
    c = np.ascontiguousarray(scaled.reshape(k // 512, 128, 4, n).transpose(0, 1, 3, 2)).astype(ml_dtypes.float4_e2m1fn).view(np.uint8) & 0xF
    words = (c[..., 0::2] | (c[..., 1::2] << 4)).reshape(k // 512, 128, 2 * n)
    return np.ascontiguousarray(words), np.ascontiguousarray(byte.astype(np.uint8).reshape(k // 512, 16, n))


def unpack_fp4(words, scales):
    g, _, n = scales.shape
    words = np.ascontiguousarray(words).reshape(g, 128, n, 2)
    nib = np.empty((g, 128, n, 4), np.uint8)
    nib[..., 0::2] = words & 0xF
    nib[..., 1::2] = words >> 4
    vals = E2M1[nib] * np.repeat(np.exp2(scales.astype(np.float64) - 127.0), 8, axis=1)[..., None]
    return vals.transpose(0, 1, 3, 2).reshape(g * 512, n)


def sigmoid(v):
    return 1.0 / (1.0 + np.exp(-np.maximum(v, -700.0)))

def planes(y):
    n, m = y.shape
    v = y.astype(np.float32).astype(ml_dtypes.bfloat16).astype(np.float64).reshape(n // 32, 32, m)
    top = np.abs(v).max(1)
    byte = np.clip(np.where(top > 0, np.frexp(top)[1] - 1 + 127 - 7, 1), 1, 254)
    codes = (v * np.exp2(127.0 - byte)[:, None, :]).reshape(n, m).astype(np.float32).astype(ml_dtypes.float8_e4m3fn).view(np.uint8)
    words = codes.reshape(n // 512, 128, 4, m).transpose(0, 1, 3, 2)
    return np.ascontiguousarray(words), np.ascontiguousarray(byte.astype(np.uint8).reshape(n // 512, 16, m))


K, T, S, N, H = 512, 2048, 512, 512, 512


def setup_inputs():
    n = np.random.standard_normal
    s = mx_kscale(K)[:, None]
    u = mx_kscale(H)
    packed_xT = pack_weight(n((K, T)) * s)
    packed_w1 = pack_fp4(n((K, H)) / np.sqrt(K) / s)
    packed_w2 = pack_fp4(n((H, N)) / np.sqrt(H) / u[:, None])
    packed_w3 = pack_fp4(n((K, N)) / np.sqrt(K) / s)
    return {
        "x_words": packed_xT[0],
        "x_scales": packed_xT[1],
        "w1_words": packed_w1[0],
        "w1_scales": packed_w1[1],
        "tau": np.random.uniform(0.3, 0.9, (H, 1)).astype(np.float32),
        "gn": (np.random.uniform(0.5, 1.5, (H, 1)) * u[:, None]).astype(np.float32),
        "w2_words": packed_w2[0],
        "w2_scales": packed_w2[1],
        "w3_words": packed_w3[0],
        "w3_scales": packed_w3[1],
        "sl": np.random.uniform(1.0, 2.0, (N, 1)).astype(np.float32),
        "th": (0.5 * n((N, 1))).astype(np.float32),
        "offs": striped(np.random.permutation(T)[:S]),
        "n1": striped8(np.stack([np.random.permutation(S) for _ in range(8)])),
        "n2": striped8(np.stack([np.random.permutation(S) for _ in range(8)])),
        "two": striped(np.random.permutation(T)[:S]),
        "n3": striped8(np.stack([np.random.permutation(S) for _ in range(8)])),
        "n4": striped8(np.stack([np.random.permutation(S) for _ in range(8)])),
    }


def reference(x_words, x_scales, w1_words, w1_scales, tau, gn, w2_words, w2_scales, w3_words, w3_scales, sl, th, offs, n1, n2, two, n3, n4):
    xq = unpack_weight(x_words, x_scales)[:, unstriped(offs)]
    y = unpack_fp4(w1_words, w1_scales).T @ xq
    top = y.max(axis=1, keepdims=True)
    ea = np.exp(f64(tau) * (y[np.arange(H)[:, None], runs(n1, H)] - top))
    sm = y * ea
    ds = np.zeros((H, S))
    ds[np.arange(H)[:, None], runs(n2, H)] = sm
    z = f64(gn) * (2.0 * ds - (0.5 * y))
    h = unpack_fp4(w2_words, w2_scales).T @ mxq(z, 0, "e4m3")
    x_two = unpack_weight(x_words, x_scales)[:, unstriped(two)]
    d = unpack_fp4(w3_words, w3_scales).T @ x_two
    sg = sigmoid(f64(sl) * (d[np.arange(N)[:, None], runs(n3, N)] - f64(th)))
    out_0 = np.maximum(h * sg, d[np.arange(N)[:, None], runs(n4, N)] - d)
    return (out_0,) + planes(out_0)

@@ -1,0 +1,236 @@
+from contextlib import ExitStack
+
+import concourse.mybir as mybir
+
+K, T, S, N, H = 512, 2048, 512, 512, 512
+FLOPS = 2 * S * (K * H + H * N + K * N)
+
+F32 = mybir.dt.float32
+BF16 = mybir.dt.bfloat16
+I32 = mybir.dt.int32
+U32 = mybir.dt.uint32
+U16 = mybir.dt.uint16
+U8 = mybir.dt.uint8
+FP8X4 = mybir.dt.float8_e4m3fn_x4
+FP4X4 = mybir.dt.float4_e2m1fn_x4
+ALU = mybir.AluOpType
+ACT = mybir.ActivationFunctionType
+
+P = 128
+PACK = 4
+WINDOW = 2 * S
+CHUNK = 128
+NCHUNK = S // CHUNK
+
+
+def tile_picked_latemxbesd_none_po_kernel(
+    tc, x_words, x_scales, w1_words, w1_scales, tau, gn, w2_words, w2_scales, w3_words, w3_scales,
+    sl, th, offs, n1, n2, two, n3, n4, out_0, out_1, out_2,
+):
+    nc = tc.nc
+    with ExitStack() as ctx:
+        keep = ctx.enter_context(tc.tile_pool(name="keep", bufs=1))
+        psum = ctx.enter_context(tc.psum_pool(name="psum", bufs=1))
+
+        def load_list(src, name):
+            t = keep.tile([P, S // 16], U16, name=name)
+            nc.sync.dma_start(t[:], src)
+            return t
+
+        def load_scale_rows(queue, dst, src):
+            for q in range(4):
+                queue.dma_start(dst[32 * q : 32 * q + 4, :].bitcast(I32), src[0, 4 * q : 4 * q + 4, :].bitcast(I32))
+
+        def load_column(src, name):
+            t = keep.tile([P, PACK], F32, name=name)
+            nc.gpsimd.dma_start(t[:], src.rearrange("(p t) o -> p (t o)", t=PACK))
+            return t
+
+        def load_words(queue, src, name):
+            t = keep.tile([P, 2 * H], U8, name=name)
+            queue.dma_start(t[:].bitcast(I32), src[0].bitcast(I32))
+            return t
+
+        xs = keep.tile([P, T], U8, name="xs")
+        nc.vector.memset(xs[:].bitcast(I32), 0)
+        wsr = [keep.tile([P, H], U8, name=f"wsr{i}") for i in range(3)]
+        nc.gpsimd.memset(wsr[0][:].bitcast(I32), 0)
+        nc.gpsimd.memset(wsr[2][:].bitcast(I32), 0)
+        nc.gpsimd.memset(wsr[1][:].bitcast(I32), 0)
+
+        l_offs = load_list(offs, "l_offs")
+        l_two = load_list(two, "l_two")
+        xw = keep.tile([P, T], U32, name="xw")
+        nc.sync.dma_start(xw[:].bitcast(I32), x_words[0].rearrange("p c r -> p (c r)").bitcast(I32))
+        w1r = load_words(nc.scalar, w1_words, "w1r")
+        load_scale_rows(nc.scalar, xs, x_scales)
+        load_scale_rows(nc.scalar, wsr[0], w1_scales)
+        tau_t = load_column(tau, "tau_t")
+        gn_t = load_column(gn, "gn_t")
+        sl_t = load_column(sl, "sl_t")
+        th_t = load_column(th, "th_t")
+        l_n1 = load_list(n1, "l_n1")
+        w3r = load_words(nc.sync, w3_words, "w3r")
+        load_scale_rows(nc.sync, wsr[2], w3_scales)
+        l_n2 = load_list(n2, "l_n2")
+        l_n4 = load_list(n4, "l_n4")
+        l_n3 = load_list(n3, "l_n3")
+        w2r = load_words(nc.sync, w2_words, "w2r")
+        load_scale_rows(nc.sync, wsr[1], w2_scales)
+
+        ntau = keep.tile([P, PACK], F32, name="ntau")
+        nc.gpsimd.tensor_scalar(ntau[:], tau_t[:], -1.0, 0.0, ALU.mult, ALU.add)
+        g_ds = keep.tile([P, PACK], F32, name="g_ds")
+        nc.gpsimd.tensor_scalar(g_ds[:], gn_t[:], 2.0, 0.0, ALU.mult, ALU.add)
+        g_y = keep.tile([P, PACK], F32, name="g_y")
+        nc.gpsimd.tensor_scalar(g_y[:], gn_t[:], -0.5, 0.0, ALU.mult, ALU.add)
+        nsl = keep.tile([P, PACK], F32, name="nsl")
+        nc.gpsimd.tensor_scalar(nsl[:], sl_t[:], -1.0, 0.0, ALU.mult, ALU.add)
+        sbias = keep.tile([P, PACK], F32, name="sbias")
+        nc.gpsimd.tensor_tensor(sbias[:], nsl[:], th_t[:], ALU.mult)
+
+        def gathered(name):
+            w = keep.tile([P, S], U32, name=name + "_w", align_bytes=64)
+            s = keep.tile([P, S], U8, name=name + "_s", align_bytes=64)
+            return w, s
+
+        xa_w, xa_s = gathered("xa")
+        xb_w, xb_s = gathered("xb")
+        wd = [keep.tile([P, 2 * H], U8, name=f"wd{i}", align_bytes=64) for i in range(3)]
+        wsd = [keep.tile([P, H], U8, name=f"wsd{i}", align_bytes=64) for i in range(3)]
+
+        def deal_scales(engine, i):
+            engine.tensor_copy(
+                wsd[i][:].rearrange("p (t m) -> p t m", t=PACK), wsr[i][:].rearrange("p (m t) -> p t m", t=PACK)
+            )
+
+        def deal_words_scalar(i, raw):
+            nc.scalar.copy(
+                wd[i][:].bitcast(U16).rearrange("p (t m) -> p t m", t=PACK),
+                raw[:].bitcast(U16).rearrange("p (m t) -> p t m", t=PACK),
+            )
+
+        nc.vector.tensor_copy(xa_s[:], xs[:].indirect(l_offs[:]))
+        nc.vector.tensor_copy(xb_s[:], xs[:].indirect(l_two[:]))
+        deal_words_scalar(0, w1r)
+        deal_scales(nc.gpsimd, 0)
+        nc.vector.tensor_copy(xa_w[:], xw[:].indirect(l_offs[:]))
+        nc.vector.tensor_copy(xb_w[:], xw[:].indirect(l_two[:]))
+        deal_words_scalar(2, w3r)
+        deal_scales(nc.gpsimd, 2)
+        deal_scales(nc.gpsimd, 1)
+
+        def product(dst, i, t, codes, scales):
+            nc.tensor.matmul_mx(
+                dst,
+                lhsT=wd[i][:, 2 * P * t : 2 * P * (t + 1)].bitcast(FP4X4),
+                lhsT_scale=wsd[i][:, P * t : P * (t + 1)],
+                rhs=codes.bitcast(FP8X4),
+                rhs_scale=scales,
+                start=True,
+                stop=True,
+            )
+
+        y_ps = [psum.tile([P, S], F32, name=f"y_ps{t}", tag=f"bank{t}") for t in range(PACK)]
+        d_ps = [psum.tile([P, S], F32, name=f"d_ps{t}", tag=f"bank{4 + t}") for t in range(PACK)]
+        for t in range(PACK):
+            product(y_ps[t][:], 0, t, xa_w[:], xa_s[:])
+        for t in range(PACK):
+            product(d_ps[t][:], 2, t, xb_w[:], xb_s[:])
+
+        y = [keep.tile([P, WINDOW], F32, name=f"y{t}", tag=f"y{t}") for t in range(PACK)]
+        yh = [keep.tile([P, S], F32, name=f"yh{t}") for t in range(PACK)]
+        ea = [keep.tile([P, S], F32, name=f"ea{t}") for t in range(PACK)]
+        top = [keep.tile([P, 1], F32, name=f"top{t}") for t in range(PACK)]
+        ebias = [keep.tile([P, 1], F32, name=f"ebias{t}") for t in range(PACK)]
+        for t in range(PACK):
+            nc.scalar.activation(yh[t][:], y_ps[t][:], ACT.Copy, scale=g_ds[:, t : t + 1])
+            nc.vector.tensor_scalar(y[t][:, 0:S], y_ps[t][:], 1.0, None, ALU.mult, ALU.max, accum_out=top[t][:])
+            nc.vector.tensor_tensor(ebias[t][:], top[t][:], ntau[:, t : t + 1], ALU.mult)
+            nc.scalar.activation(
+                ea[t][:], y[t][:].indirect(l_n1[:]), ACT.Exp, bias=ebias[t][:], scale=tau_t[:, t : t + 1]
+            )
+
+        d = [keep.tile([P, WINDOW], F32, name=f"d{t}") for t in range(PACK)]
+        dg = [keep.tile([P, S], F32, name=f"dg{t}") for t in range(PACK)]
+        for t in range(PACK):
+            nc.scalar.copy(d[t][:, 0:S], d_ps[t][:])
+            nc.scalar.activation(dg[t][:], d[t][:].indirect(l_n4[:]), ACT.Copy)
+        deal_words_scalar(1, w2r)
+        sg = keep.tile([P, PACK, S], F32, name="sg", tag=f"y{PACK - 1}")
+        for t in range(PACK):
+            nc.scalar.activation(
+                sg[:, t, :], d[t][:].indirect(l_n3[:]), ACT.Sigmoid, bias=sbias[:, t : t + 1], scale=sl_t[:, t : t + 1]
+            )
+
+        ds = [keep.tile([P, WINDOW], F32, name=f"ds{t}") for t in range(PACK)]
+        zp = keep.tile([P, PACK, S], BF16, name="zp")
+        e = keep.tile([P, PACK, S], F32, name="e")
+
+        def make_z(t, cols):
+            nc.vector.scalar_tensor_tensor(
+                zp[:, t, cols], y_ps[t][:, cols], g_y[:, t : t + 1], ds[t][:, cols], ALU.mult, ALU.add
+            )
+
+        def make_e(t):
+            nc.vector.tensor_tensor(e[:, t, :], dg[t][:], d_ps[t][:], ALU.subtract)
+
+        for t in range(PACK):
+            nc.vector.tensor_tensor(ds[t][:].indirect(l_n2[:]), yh[t][:], ea[t][:], ALU.mult)
+            if t > 0:
+                make_z(t - 1, slice(0, S))
+            if t > 1:
+                make_e(t - 2)
+
+        chunks = [slice(c * CHUNK, (c + 1) * CHUNK) for c in range(NCHUNK)]
+
+        def interleave(copy, dst, src):
+            copy(
+                dst[:].rearrange("p (c i t) -> p c t i", i=4, t=PACK),
+                src.rearrange("p t (c i) -> p c t i", i=4),
+            )
+
+        zi = [keep.tile([P, PACK * CHUNK], BF16, name=f"zi{c}", align_bytes=64) for c in range(NCHUNK)]
+        oi = [keep.tile([P, PACK * CHUNK], BF16, name=f"oi{c}", align_bytes=64) for c in range(NCHUNK)]
+        zq_w = [keep.tile([P, CHUNK], U32, name=f"zq_w{c}", align_bytes=64) for c in range(NCHUNK)]
+        zq_s = [keep.tile([P, CHUNK], U8, name=f"zq_s{c}", align_bytes=64) for c in range(NCHUNK)]
+        oq_w = keep.tile([P, S], U32, name="oq_w", align_bytes=64)
+        oq_s = keep.tile([P, S], U8, name="oq_s", align_bytes=64)
+        hs = [keep.tile([P, PACK, CHUNK], F32, name=f"hs{c}") for c in range(NCHUNK)]
+        res = [keep.tile([P, PACK, CHUNK], F32, name=f"res{c}") for c in range(NCHUNK)]
+        h_ps = [psum.tile([P, PACK, CHUNK], F32, name=f"h_ps{c}", tag=f"bank{c}") for c in range(NCHUNK)]
+        out_rows = out_0.rearrange("(p t) c -> p t c", t=PACK)
+        out_words = out_1[0].rearrange("p c r -> p (c r)").bitcast(I32)
+
+        for c in range(NCHUNK):
+            make_z(PACK - 1, chunks[c])
+            interleave(nc.scalar.copy, zi[c], zp[:, :, chunks[c]])
+        make_e(PACK - 2)
+
+        def second_product(c):
+            nc.vector.quantize_mx(zq_w[c][:].bitcast(FP8X4), zq_s[c][:], zi[c][:])
+            for t in range(PACK):
+                product(h_ps[c][:, t, :], 1, t, zq_w[c][:], zq_s[c][:])
+
+        def combine(c):
+            nc.vector.tensor_tensor(hs[c][:], h_ps[c][:], sg[:, :, chunks[c]], ALU.mult)
+            nc.vector.tensor_tensor(res[c][:], hs[c][:], e[:, :, chunks[c]], ALU.max)
+            nc.sync.dma_start(out_rows[:, :, chunks[c]], res[c][:])
+            interleave(nc.scalar.copy if c < NCHUNK - 1 else nc.vector.tensor_copy, oi[c], res[c][:])
+
+        def planes(c):
+            nc.vector.quantize_mx(oq_w[:, chunks[c]].bitcast(FP8X4), oq_s[:, chunks[c]], oi[c][:])
+            nc.sync.dma_start(out_words[:, chunks[c]], oq_w[:, chunks[c]].bitcast(I32))
+
+        second_product(0)
+        make_e(PACK - 1)
+        for c in range(NCHUNK):
+            if c + 1 < NCHUNK:
+                second_product(c + 1)
+            combine(c)
+            if c > 0:
+                planes(c - 1)
+        planes(NCHUNK - 1)
+        for q in range(4):
+            queue = nc.scalar if q % 2 == 0 else nc.sync
+            queue.dma_start(out_2[0, 4 * q : 4 * q + 4, :].bitcast(I32), oq_s[32 * q : 32 * q + 4, :].bitcast(I32))

@@ -41,9 +41,9 @@ def tile_picked_latemxbesd_none_po_kernel(
             for q in range(4):
                 queue.dma_start(dst[32 * q : 32 * q + 4, :].bitcast(I32), src[0, 4 * q : 4 * q + 4, :].bitcast(I32))
 
-        def load_column(src, name):
+        def load_column(queue, src, name):
             t = keep.tile([P, PACK], F32, name=name)
-            nc.gpsimd.dma_start(t[:], src.rearrange("(p t) o -> p (t o)", t=PACK))
+            queue.dma_start(t[:], src.rearrange("(p t) o -> p (t o)", t=PACK))
             return t
 
         def load_words(queue, src, name):
@@ -53,41 +53,29 @@ def tile_picked_latemxbesd_none_po_kernel(
 
         xs = keep.tile([P, T], U8, name="xs")
         nc.vector.memset(xs[:].bitcast(I32), 0)
-        wsr = [keep.tile([P, H], U8, name=f"wsr{i}") for i in range(3)]
-        nc.gpsimd.memset(wsr[0][:].bitcast(I32), 0)
-        nc.gpsimd.memset(wsr[2][:].bitcast(I32), 0)
-        nc.gpsimd.memset(wsr[1][:].bitcast(I32), 0)
+        wsr = [keep.tile([P, H], U8, name=f"wsr{i}", tag=f"wsr{i}") for i in range(3)]
+        for i in (0, 2, 1):
+            nc.gpsimd.memset(wsr[i][:].bitcast(I32), 0)
 
         l_offs = load_list(offs, "l_offs")
         l_two = load_list(two, "l_two")
+        load_scale_rows(nc.sync, xs, x_scales)
         xw = keep.tile([P, T], U32, name="xw")
         nc.sync.dma_start(xw[:].bitcast(I32), x_words[0].rearrange("p c r -> p (c r)").bitcast(I32))
-        w1r = load_words(nc.scalar, w1_words, "w1r")
-        load_scale_rows(nc.scalar, xs, x_scales)
-        load_scale_rows(nc.scalar, wsr[0], w1_scales)
-        tau_t = load_column(tau, "tau_t")
-        gn_t = load_column(gn, "gn_t")
-        sl_t = load_column(sl, "sl_t")
-        th_t = load_column(th, "th_t")
+        w1r = load_words(nc.sync, w1_words, "w1r")
+        load_scale_rows(nc.sync, wsr[0], w1_scales)
+        tau_t = load_column(nc.gpsimd, tau, "tau_t")
+        gn_t = load_column(nc.gpsimd, gn, "gn_t")
+        sl_t = load_column(nc.gpsimd, sl, "sl_t")
+        th_t = load_column(nc.gpsimd, th, "th_t")
         l_n1 = load_list(n1, "l_n1")
         w3r = load_words(nc.sync, w3_words, "w3r")
         load_scale_rows(nc.sync, wsr[2], w3_scales)
         l_n2 = load_list(n2, "l_n2")
         l_n4 = load_list(n4, "l_n4")
-        l_n3 = load_list(n3, "l_n3")
         w2r = load_words(nc.sync, w2_words, "w2r")
         load_scale_rows(nc.sync, wsr[1], w2_scales)
-
-        ntau = keep.tile([P, PACK], F32, name="ntau")
-        nc.gpsimd.tensor_scalar(ntau[:], tau_t[:], -1.0, 0.0, ALU.mult, ALU.add)
-        g_ds = keep.tile([P, PACK], F32, name="g_ds")
-        nc.gpsimd.tensor_scalar(g_ds[:], gn_t[:], 2.0, 0.0, ALU.mult, ALU.add)
-        g_y = keep.tile([P, PACK], F32, name="g_y")
-        nc.gpsimd.tensor_scalar(g_y[:], gn_t[:], -0.5, 0.0, ALU.mult, ALU.add)
-        nsl = keep.tile([P, PACK], F32, name="nsl")
-        nc.gpsimd.tensor_scalar(nsl[:], sl_t[:], -1.0, 0.0, ALU.mult, ALU.add)
-        sbias = keep.tile([P, PACK], F32, name="sbias")
-        nc.gpsimd.tensor_tensor(sbias[:], nsl[:], th_t[:], ALU.mult)
+        l_n3 = load_list(n3, "l_n3")
 
         def gathered(name):
             w = keep.tile([P, S], U32, name=name + "_w", align_bytes=64)
@@ -116,9 +104,16 @@ def tile_picked_latemxbesd_none_po_kernel(
         deal_scales(nc.gpsimd, 0)
         nc.vector.tensor_copy(xa_w[:], xw[:].indirect(l_offs[:]))
         nc.vector.tensor_copy(xb_w[:], xw[:].indirect(l_two[:]))
+        g_y = keep.tile([P, PACK], F32, name="g_y")
+        nc.scalar.activation(g_y[:], gn_t[:], ACT.Copy, scale=-0.5)
+        g_ds = keep.tile([P, 1], F32, name="g_ds")
+        nc.scalar.activation(g_ds[:], gn_t[:, 0:1], ACT.Copy, scale=2.0)
         deal_words_scalar(2, w3r)
         deal_scales(nc.gpsimd, 2)
-        deal_scales(nc.gpsimd, 1)
+        nsl = keep.tile([P, PACK], F32, name="nsl", tag="wsr2")
+        nc.gpsimd.tensor_scalar(nsl[:], sl_t[:], -1.0, 0.0, ALU.mult, ALU.add)
+        sbias = keep.tile([P, PACK], F32, name="sbias", tag="sbias", align_bytes=64)
+        nc.gpsimd.tensor_tensor(sbias[:], nsl[:], th_t[:], ALU.mult)
 
         def product(dst, i, t, codes, scales):
             nc.tensor.matmul_mx(
@@ -139,24 +134,34 @@ def tile_picked_latemxbesd_none_po_kernel(
             product(d_ps[t][:], 2, t, xb_w[:], xb_s[:])
 
         y = [keep.tile([P, WINDOW], F32, name=f"y{t}", tag=f"y{t}") for t in range(PACK)]
-        yh = [keep.tile([P, S], F32, name=f"yh{t}") for t in range(PACK)]
+        y2 = [keep.tile([P, S], F32, name=f"y2_{t}") for t in range(1, PACK)]
+        sm = [keep.tile([P, S], F32, name=f"sm{t}") for t in range(PACK)]
         ea = [keep.tile([P, S], F32, name=f"ea{t}") for t in range(PACK)]
         top = [keep.tile([P, 1], F32, name=f"top{t}") for t in range(PACK)]
         ebias = [keep.tile([P, 1], F32, name=f"ebias{t}") for t in range(PACK)]
         for t in range(PACK):
-            nc.scalar.activation(yh[t][:], y_ps[t][:], ACT.Copy, scale=g_ds[:, t : t + 1])
             nc.vector.tensor_scalar(y[t][:, 0:S], y_ps[t][:], 1.0, None, ALU.mult, ALU.max, accum_out=top[t][:])
-            nc.vector.tensor_tensor(ebias[t][:], top[t][:], ntau[:, t : t + 1], ALU.mult)
+            nc.vector.tensor_scalar(ebias[t][:], top[t][:], tau_t[:, t : t + 1], -1.0, ALU.mult, ALU.mult)
             nc.scalar.activation(
                 ea[t][:], y[t][:].indirect(l_n1[:]), ACT.Exp, bias=ebias[t][:], scale=tau_t[:, t : t + 1]
             )
+        nc.vector.scalar_tensor_tensor(sm[0][:], y_ps[0][:], g_ds[:], ea[0][:], ALU.mult, ALU.mult)
+        for t in range(1, PACK):
+            nc.gpsimd.tensor_scalar(y2[t - 1][:], y[t][:, 0:S], gn_t[:, t : t + 1], 2.0, ALU.mult, ALU.mult)
+            nc.gpsimd.tensor_tensor(sm[t][:], y2[t - 1][:], ea[t][:], ALU.mult)
 
         d = [keep.tile([P, WINDOW], F32, name=f"d{t}") for t in range(PACK)]
         dg = [keep.tile([P, S], F32, name=f"dg{t}") for t in range(PACK)]
+        e = keep.tile([P, PACK, S], F32, name="e")
         for t in range(PACK):
             nc.scalar.copy(d[t][:, 0:S], d_ps[t][:])
             nc.scalar.activation(dg[t][:], d[t][:].indirect(l_n4[:]), ACT.Copy)
-        deal_words_scalar(1, w2r)
+            nc.gpsimd.tensor_tensor(e[:, t, :], dg[t][:], d[t][:, 0:S], ALU.subtract)
+        nc.gpsimd.tensor_copy(
+            wd[1][:].rearrange("p (t m b) -> p t m b", t=PACK, b=2),
+            w2r[:].rearrange("p (m t b) -> p t m b", t=PACK, b=2),
+        )
+        deal_scales(nc.gpsimd, 1)
         sg = keep.tile([P, PACK, S], F32, name="sg", tag=f"y{PACK - 1}")
         for t in range(PACK):
             nc.scalar.activation(
@@ -165,32 +170,27 @@ def tile_picked_latemxbesd_none_po_kernel(
 
         ds = [keep.tile([P, WINDOW], F32, name=f"ds{t}") for t in range(PACK)]
         zp = keep.tile([P, PACK, S], BF16, name="zp")
-        e = keep.tile([P, PACK, S], F32, name="e")
 
         def make_z(t, cols):
             nc.vector.scalar_tensor_tensor(
                 zp[:, t, cols], y_ps[t][:, cols], g_y[:, t : t + 1], ds[t][:, cols], ALU.mult, ALU.add
             )
 
-        def make_e(t):
-            nc.vector.tensor_tensor(e[:, t, :], dg[t][:], d_ps[t][:], ALU.subtract)
-
         for t in range(PACK):
-            nc.vector.tensor_tensor(ds[t][:].indirect(l_n2[:]), yh[t][:], ea[t][:], ALU.mult)
+            nc.vector.tensor_copy(ds[t][:].indirect(l_n2[:]), sm[t][:])
             if t > 0:
                 make_z(t - 1, slice(0, S))
-            if t > 1:
-                make_e(t - 2)
 
         chunks = [slice(c * CHUNK, (c + 1) * CHUNK) for c in range(NCHUNK)]
 
         def interleave(copy, dst, src):
             copy(
-                dst[:].rearrange("p (c i t) -> p c t i", i=4, t=PACK),
+                dst.rearrange("p (c i t) -> p c t i", i=4, t=PACK),
                 src.rearrange("p t (c i) -> p c t i", i=4),
             )
 
-        zi = [keep.tile([P, PACK * CHUNK], BF16, name=f"zi{c}", align_bytes=64) for c in range(NCHUNK)]
+        zi_all = keep.tile([P, PACK * S], BF16, name="zi_all", tag="sbias", align_bytes=64)
+        zi = [zi_all[:, PACK * CHUNK * c : PACK * CHUNK * (c + 1)] for c in range(NCHUNK)]
         oi = [keep.tile([P, PACK * CHUNK], BF16, name=f"oi{c}", align_bytes=64) for c in range(NCHUNK)]
         zq_w = [keep.tile([P, CHUNK], U32, name=f"zq_w{c}", align_bytes=64) for c in range(NCHUNK)]
         zq_s = [keep.tile([P, CHUNK], U8, name=f"zq_s{c}", align_bytes=64) for c in range(NCHUNK)]
@@ -198,17 +198,16 @@ def tile_picked_latemxbesd_none_po_kernel(
         oq_s = keep.tile([P, S], U8, name="oq_s", align_bytes=64)
         hs = [keep.tile([P, PACK, CHUNK], F32, name=f"hs{c}") for c in range(NCHUNK)]
         res = [keep.tile([P, PACK, CHUNK], F32, name=f"res{c}") for c in range(NCHUNK)]
-        h_ps = [psum.tile([P, PACK, CHUNK], F32, name=f"h_ps{c}", tag=f"bank{c}") for c in range(NCHUNK)]
+        h_ps = [psum.tile([P, PACK, CHUNK], F32, name=f"h_ps{c}", tag=f"bank{4 + c}") for c in range(NCHUNK)]
         out_rows = out_0.rearrange("(p t) c -> p t c", t=PACK)
         out_words = out_1[0].rearrange("p c r -> p (c r)").bitcast(I32)
 
         for c in range(NCHUNK):
             make_z(PACK - 1, chunks[c])
             interleave(nc.scalar.copy, zi[c], zp[:, :, chunks[c]])
-        make_e(PACK - 2)
 
         def second_product(c):
-            nc.vector.quantize_mx(zq_w[c][:].bitcast(FP8X4), zq_s[c][:], zi[c][:])
+            nc.vector.quantize_mx(zq_w[c][:].bitcast(FP8X4), zq_s[c][:], zi[c])
             for t in range(PACK):
                 product(h_ps[c][:, t, :], 1, t, zq_w[c][:], zq_s[c][:])
 
@@ -216,14 +215,13 @@ def tile_picked_latemxbesd_none_po_kernel(
             nc.vector.tensor_tensor(hs[c][:], h_ps[c][:], sg[:, :, chunks[c]], ALU.mult)
             nc.vector.tensor_tensor(res[c][:], hs[c][:], e[:, :, chunks[c]], ALU.max)
             nc.sync.dma_start(out_rows[:, :, chunks[c]], res[c][:])
-            interleave(nc.scalar.copy if c < NCHUNK - 1 else nc.vector.tensor_copy, oi[c], res[c][:])
+            interleave(nc.scalar.copy if c < NCHUNK - 1 else nc.vector.tensor_copy, oi[c][:], res[c][:])
 
         def planes(c):
             nc.vector.quantize_mx(oq_w[:, chunks[c]].bitcast(FP8X4), oq_s[:, chunks[c]], oi[c][:])
             nc.sync.dma_start(out_words[:, chunks[c]], oq_w[:, chunks[c]].bitcast(I32))
 
         second_product(0)
-        make_e(PACK - 1)
         for c in range(NCHUNK):
             if c + 1 < NCHUNK:
                 second_product(c + 1)

@@ -37,9 +37,9 @@ def tile_picked_latemxbesd_none_po_kernel(
             nc.sync.dma_start(t[:], src)
             return t
 
-        def load_scale_rows(queue, dst, src):
+        def load_scale_rows(queues, dst, src):
             for q in range(4):
-                queue.dma_start(dst[32 * q : 32 * q + 4, :].bitcast(I32), src[0, 4 * q : 4 * q + 4, :].bitcast(I32))
+                queues[q // 2].dma_start(dst[32 * q : 32 * q + 4, :].bitcast(I32), src[0, 4 * q : 4 * q + 4, :].bitcast(I32))
 
         def load_column(queue, src, name):
             t = keep.tile([P, PACK], F32, name=name)
@@ -59,22 +59,22 @@ def tile_picked_latemxbesd_none_po_kernel(
 
         l_offs = load_list(offs, "l_offs")
         l_two = load_list(two, "l_two")
-        load_scale_rows(nc.sync, xs, x_scales)
+        load_scale_rows((nc.sync, nc.scalar), xs, x_scales)
         xw = keep.tile([P, T], U32, name="xw")
         nc.sync.dma_start(xw[:].bitcast(I32), x_words[0].rearrange("p c r -> p (c r)").bitcast(I32))
         w1r = load_words(nc.sync, w1_words, "w1r")
-        load_scale_rows(nc.sync, wsr[0], w1_scales)
+        load_scale_rows((nc.sync, nc.sync), wsr[0], w1_scales)
         tau_t = load_column(nc.gpsimd, tau, "tau_t")
         gn_t = load_column(nc.gpsimd, gn, "gn_t")
         sl_t = load_column(nc.gpsimd, sl, "sl_t")
         th_t = load_column(nc.gpsimd, th, "th_t")
         l_n1 = load_list(n1, "l_n1")
         w3r = load_words(nc.sync, w3_words, "w3r")
-        load_scale_rows(nc.sync, wsr[2], w3_scales)
+        w2r = load_words(nc.sync, w2_words, "w2r")
+        load_scale_rows((nc.sync, nc.sync), wsr[2], w3_scales)
         l_n2 = load_list(n2, "l_n2")
         l_n4 = load_list(n4, "l_n4")
-        w2r = load_words(nc.sync, w2_words, "w2r")
-        load_scale_rows(nc.sync, wsr[1], w2_scales)
+        load_scale_rows((nc.sync, nc.sync), wsr[1], w2_scales)
         l_n3 = load_list(n3, "l_n3")
 
         def gathered(name):
@@ -109,6 +109,7 @@ def tile_picked_latemxbesd_none_po_kernel(
         g_ds = keep.tile([P, 1], F32, name="g_ds")
         nc.scalar.activation(g_ds[:], gn_t[:, 0:1], ACT.Copy, scale=2.0)
         deal_words_scalar(2, w3r)
+        deal_words_scalar(1, w2r)
         deal_scales(nc.gpsimd, 2)
         nsl = keep.tile([P, PACK], F32, name="nsl", tag="wsr2")
         nc.gpsimd.tensor_scalar(nsl[:], sl_t[:], -1.0, 0.0, ALU.mult, ALU.add)
@@ -141,7 +142,7 @@ def tile_picked_latemxbesd_none_po_kernel(
         ebias = [keep.tile([P, 1], F32, name=f"ebias{t}") for t in range(PACK)]
         for t in range(PACK):
             nc.vector.tensor_scalar(y[t][:, 0:S], y_ps[t][:], 1.0, None, ALU.mult, ALU.max, accum_out=top[t][:])
-            nc.vector.tensor_scalar(ebias[t][:], top[t][:], tau_t[:, t : t + 1], -1.0, ALU.mult, ALU.mult)
+            nc.gpsimd.tensor_scalar(ebias[t][:], top[t][:], tau_t[:, t : t + 1], -1.0, ALU.mult, ALU.mult)
             nc.scalar.activation(
                 ea[t][:], y[t][:].indirect(l_n1[:]), ACT.Exp, bias=ebias[t][:], scale=tau_t[:, t : t + 1]
             )
@@ -157,10 +158,6 @@ def tile_picked_latemxbesd_none_po_kernel(
             nc.scalar.copy(d[t][:, 0:S], d_ps[t][:])
             nc.scalar.activation(dg[t][:], d[t][:].indirect(l_n4[:]), ACT.Copy)
             nc.gpsimd.tensor_tensor(e[:, t, :], dg[t][:], d[t][:, 0:S], ALU.subtract)
-        nc.gpsimd.tensor_copy(
-            wd[1][:].rearrange("p (t m b) -> p t m b", t=PACK, b=2),
-            w2r[:].rearrange("p (m t b) -> p t m b", t=PACK, b=2),
-        )
         deal_scales(nc.gpsimd, 1)
         sg = keep.tile([P, PACK, S], F32, name="sg", tag=f"y{PACK - 1}")
         for t in range(PACK):
@@ -189,8 +186,9 @@ def tile_picked_latemxbesd_none_po_kernel(
                 src.rearrange("p t (c i) -> p c t i", i=4),
             )
 
-        zi_all = keep.tile([P, PACK * S], BF16, name="zi_all", tag="sbias", align_bytes=64)
-        zi = [zi_all[:, PACK * CHUNK * c : PACK * CHUNK * (c + 1)] for c in range(NCHUNK)]
+        zi_first = keep.tile([P, 2, PACK * CHUNK], BF16, name="zi_first", align_bytes=64)
+        zi_rest = keep.tile([P, 2, PACK * CHUNK], BF16, name="zi_rest", tag="sbias", align_bytes=64)
+        zi = [zi_first[:, 0, :], zi_first[:, 1, :], zi_rest[:, 0, :], zi_rest[:, 1, :]]
         oi = [keep.tile([P, PACK * CHUNK], BF16, name=f"oi{c}", align_bytes=64) for c in range(NCHUNK)]
         zq_w = [keep.tile([P, CHUNK], U32, name=f"zq_w{c}", align_bytes=64) for c in range(NCHUNK)]
         zq_s = [keep.tile([P, CHUNK], U8, name=f"zq_s{c}", align_bytes=64) for c in range(NCHUNK)]
@@ -202,33 +200,48 @@ def tile_picked_latemxbesd_none_po_kernel(
         out_rows = out_0.rearrange("(p t) c -> p t c", t=PACK)
         out_words = out_1[0].rearrange("p c r -> p (c r)").bitcast(I32)
 
-        for c in range(NCHUNK):
-            make_z(PACK - 1, chunks[c])
-            interleave(nc.scalar.copy, zi[c], zp[:, :, chunks[c]])
-
         def second_product(c):
             nc.vector.quantize_mx(zq_w[c][:].bitcast(FP8X4), zq_s[c][:], zi[c])
             for t in range(PACK):
                 product(h_ps[c][:, t, :], 1, t, zq_w[c][:], zq_s[c][:])
 
-        def combine(c):
+        def gate(c):
             nc.vector.tensor_tensor(hs[c][:], h_ps[c][:], sg[:, :, chunks[c]], ALU.mult)
+
+        def combine(c):
             nc.vector.tensor_tensor(res[c][:], hs[c][:], e[:, :, chunks[c]], ALU.max)
             nc.sync.dma_start(out_rows[:, :, chunks[c]], res[c][:])
-            interleave(nc.scalar.copy if c < NCHUNK - 1 else nc.vector.tensor_copy, oi[c][:], res[c][:])
+            if c < NCHUNK - 1:
+                interleave(nc.scalar.copy, oi[c][:], res[c][:])
 
         def planes(c):
             nc.vector.quantize_mx(oq_w[:, chunks[c]].bitcast(FP8X4), oq_s[:, chunks[c]], oi[c][:])
             nc.sync.dma_start(out_words[:, chunks[c]], oq_w[:, chunks[c]].bitcast(I32))
 
+        make_z(PACK - 1, chunks[0])
+        make_z(PACK - 1, chunks[1])
+        interleave(nc.vector.tensor_copy, zi[0], zp[:, :, chunks[0]])
+        make_z(PACK - 1, slice(2 * CHUNK, S))
         second_product(0)
-        for c in range(NCHUNK):
-            if c + 1 < NCHUNK:
-                second_product(c + 1)
-            combine(c)
-            if c > 0:
-                planes(c - 1)
-        planes(NCHUNK - 1)
+        interleave(nc.vector.tensor_copy, zi[1], zp[:, :, chunks[1]])
+        for c in (2, 3):
+            interleave(nc.scalar.copy, zi[c], zp[:, :, chunks[c]])
+        second_product(1)
+        gate(0)
+        second_product(2)
+        gate(1)
+        combine(0)
+        second_product(3)
+        gate(2)
+        combine(1)
+        gate(3)
+        combine(2)
+        planes(0)
+        combine(3)
+        planes(1)
+        interleave(nc.vector.tensor_copy, oi[3][:], res[3][:])
+        planes(2)
+        planes(3)
         for q in range(4):
             queue = nc.scalar if q % 2 == 0 else nc.sync
             queue.dma_start(out_2[0, 4 * q : 4 * q + 4, :].bitcast(I32), oq_s[32 * q : 32 * q + 4, :].bitcast(I32))

@@ -137,7 +137,7 @@ def tile_picked_latemxbesd_none_po_kernel(
         y = [keep.tile([P, WINDOW], F32, name=f"y{t}", tag=f"y{t}") for t in range(PACK)]
         y2 = [keep.tile([P, S], F32, name=f"y2_{t}") for t in range(1, PACK)]
         sm = [keep.tile([P, S], F32, name=f"sm{t}") for t in range(PACK)]
-        ea = [keep.tile([P, S], F32, name=f"ea{t}") for t in range(PACK)]
+        ea = [keep.tile([P, S], F32, name=f"ea{t}", tag=f"ea{t}") for t in range(PACK)]
         top = [keep.tile([P, 1], F32, name=f"top{t}") for t in range(PACK)]
         ebias = [keep.tile([P, 1], F32, name=f"ebias{t}") for t in range(PACK)]
         for t in range(PACK):
@@ -150,6 +150,13 @@ def tile_picked_latemxbesd_none_po_kernel(
         for t in range(1, PACK):
             nc.gpsimd.tensor_scalar(y2[t - 1][:], y[t][:, 0:S], gn_t[:, t : t + 1], 2.0, ALU.mult, ALU.mult)
             nc.gpsimd.tensor_tensor(sm[t][:], y2[t - 1][:], ea[t][:], ALU.mult)
+
+        ds = [keep.tile([P, WINDOW], F32, name=f"ds{t}") for t in range(PACK)]
+        zp = keep.tile([P, PACK, S], BF16, name="zp")
+        nc.vector.tensor_copy(ds[0][:].indirect(l_n2[:]), sm[0][:])
+        yneg = keep.tile([P, S], F32, name="yneg", tag=f"ea{PACK - 1}")
+        nc.gpsimd.tensor_scalar(yneg[:], y[0][:, 0:S], gn_t[:, 0:1], -0.5, ALU.mult, ALU.mult)
+        nc.gpsimd.tensor_tensor(zp[:, 0, :], ds[0][:, 0:S], yneg[:], ALU.add)
 
         d = [keep.tile([P, WINDOW], F32, name=f"d{t}") for t in range(PACK)]
         dg = [keep.tile([P, S], F32, name=f"dg{t}") for t in range(PACK)]
@@ -165,17 +172,14 @@ def tile_picked_latemxbesd_none_po_kernel(
                 sg[:, t, :], d[t][:].indirect(l_n3[:]), ACT.Sigmoid, bias=sbias[:, t : t + 1], scale=sl_t[:, t : t + 1]
             )
 
-        ds = [keep.tile([P, WINDOW], F32, name=f"ds{t}") for t in range(PACK)]
-        zp = keep.tile([P, PACK, S], BF16, name="zp")
-
         def make_z(t, cols):
             nc.vector.scalar_tensor_tensor(
                 zp[:, t, cols], y_ps[t][:, cols], g_y[:, t : t + 1], ds[t][:, cols], ALU.mult, ALU.add
             )
 
-        for t in range(PACK):
+        for t in range(1, PACK):
             nc.vector.tensor_copy(ds[t][:].indirect(l_n2[:]), sm[t][:])
-            if t > 0:
+            if t > 1:
                 make_z(t - 1, slice(0, S))
 
         chunks = [slice(c * CHUNK, (c + 1) * CHUNK) for c in range(NCHUNK)]

@@ -17,10 +17,14 @@ ALU = mybir.AluOpType
 ACT = mybir.ActivationFunctionType
 
 P = 128
-PACK = 4
+SLOTS = 4
+LAST = SLOTS - 1
+QUADRANTS = 4
+LIST_COLS = S // 16
 WINDOW = 2 * S
 CHUNK = 128
-NCHUNK = S // CHUNK
+CHUNKS = S // CHUNK
+W1, W2, W3 = 0, 1, 2
 
 
 def tile_picked_latemxbesd_none_po_kernel(
@@ -33,219 +37,230 @@ def tile_picked_latemxbesd_none_po_kernel(
         psum = ctx.enter_context(tc.psum_pool(name="psum", bufs=1))
 
         def load_list(src, name):
-            t = keep.tile([P, S // 16], U16, name=name)
-            nc.sync.dma_start(t[:], src)
-            return t
+            tile = keep.tile([P, LIST_COLS], U16, name=name)
+            nc.sync.dma_start(tile[:], src)
+            return tile
 
         def load_scale_rows(queues, dst, src):
-            for q in range(4):
-                queues[q // 2].dma_start(dst[32 * q : 32 * q + 4, :].bitcast(I32), src[0, 4 * q : 4 * q + 4, :].bitcast(I32))
+            for q in range(QUADRANTS):
+                queues[q // 2].dma_start(
+                    dst[32 * q : 32 * q + 4, :].bitcast(I32), src[0, 4 * q : 4 * q + 4, :].bitcast(I32)
+                )
 
-        def load_column(queue, src, name):
-            t = keep.tile([P, PACK], F32, name=name)
-            queue.dma_start(t[:], src.rearrange("(p t) o -> p (t o)", t=PACK))
-            return t
+        def load_row_values(src, name):
+            tile = keep.tile([P, SLOTS], F32, name=name)
+            nc.gpsimd.dma_start(tile[:], src.rearrange("(p r) o -> p (r o)", r=SLOTS))
+            return tile
 
-        def load_words(queue, src, name):
-            t = keep.tile([P, 2 * H], U8, name=name)
-            queue.dma_start(t[:].bitcast(I32), src[0].bitcast(I32))
-            return t
+        def load_weight_words(src, name):
+            tile = keep.tile([P, 2 * H], U8, name=name)
+            nc.sync.dma_start(tile[:].bitcast(I32), src[0].bitcast(I32))
+            return tile
 
-        xs = keep.tile([P, T], U8, name="xs")
-        nc.vector.memset(xs[:].bitcast(I32), 0)
-        wsr = [keep.tile([P, H], U8, name=f"wsr{i}", tag=f"wsr{i}") for i in range(3)]
-        for i in (0, 2, 1):
-            nc.gpsimd.memset(wsr[i][:].bitcast(I32), 0)
+        x_sc = keep.tile([P, T], U8, name="x_sc")
+        nc.vector.memset(x_sc[:].bitcast(I32), 0)
+        raw_sc = [keep.tile([P, H], U8, name=f"raw_sc{w}", tag=f"raw_sc{w}") for w in (W1, W2, W3)]
+        for w in (W1, W3, W2):
+            nc.gpsimd.memset(raw_sc[w][:].bitcast(I32), 0)
 
-        l_offs = load_list(offs, "l_offs")
-        l_two = load_list(two, "l_two")
-        load_scale_rows((nc.sync, nc.scalar), xs, x_scales)
-        xw = keep.tile([P, T], U32, name="xw")
-        nc.sync.dma_start(xw[:].bitcast(I32), x_words[0].rearrange("p c r -> p (c r)").bitcast(I32))
-        w1r = load_words(nc.sync, w1_words, "w1r")
-        load_scale_rows((nc.sync, nc.sync), wsr[0], w1_scales)
-        tau_t = load_column(nc.gpsimd, tau, "tau_t")
-        gn_t = load_column(nc.gpsimd, gn, "gn_t")
-        sl_t = load_column(nc.gpsimd, sl, "sl_t")
-        th_t = load_column(nc.gpsimd, th, "th_t")
-        l_n1 = load_list(n1, "l_n1")
-        w3r = load_words(nc.sync, w3_words, "w3r")
-        w2r = load_words(nc.sync, w2_words, "w2r")
-        load_scale_rows((nc.sync, nc.sync), wsr[2], w3_scales)
-        l_n2 = load_list(n2, "l_n2")
-        l_n4 = load_list(n4, "l_n4")
-        load_scale_rows((nc.sync, nc.sync), wsr[1], w2_scales)
-        l_n3 = load_list(n3, "l_n3")
+        list_offs = load_list(offs, "list_offs")
+        list_two = load_list(two, "list_two")
+        load_scale_rows((nc.sync, nc.scalar), x_sc, x_scales)
+        x_wd = keep.tile([P, T], U32, name="x_wd")
+        nc.sync.dma_start(x_wd[:].bitcast(I32), x_words[0].rearrange("p c r -> p (c r)").bitcast(I32))
+        raw_w1 = load_weight_words(w1_words, "raw_w1")
+        load_scale_rows((nc.sync, nc.sync), raw_sc[W1], w1_scales)
+        tau_sb = load_row_values(tau, "tau_sb")
+        gn_sb = load_row_values(gn, "gn_sb")
+        sl_sb = load_row_values(sl, "sl_sb")
+        th_sb = load_row_values(th, "th_sb")
+        list_n1 = load_list(n1, "list_n1")
+        raw_w3 = load_weight_words(w3_words, "raw_w3")
+        raw_w2 = load_weight_words(w2_words, "raw_w2")
+        load_scale_rows((nc.sync, nc.sync), raw_sc[W3], w3_scales)
+        list_n2 = load_list(n2, "list_n2")
+        list_n4 = load_list(n4, "list_n4")
+        load_scale_rows((nc.sync, nc.sync), raw_sc[W2], w2_scales)
+        list_n3 = load_list(n3, "list_n3")
 
-        def gathered(name):
-            w = keep.tile([P, S], U32, name=name + "_w", align_bytes=64)
-            s = keep.tile([P, S], U8, name=name + "_s", align_bytes=64)
-            return w, s
+        offs_wd = keep.tile([P, S], U32, name="offs_wd", align_bytes=64)
+        offs_sc = keep.tile([P, S], U8, name="offs_sc", align_bytes=64)
+        two_wd = keep.tile([P, S], U32, name="two_wd", align_bytes=64)
+        two_sc = keep.tile([P, S], U8, name="two_sc", align_bytes=64)
+        w_wd = [keep.tile([P, 2 * H], U8, name=f"w_wd{w}", align_bytes=64) for w in (W1, W2, W3)]
+        w_sc = [keep.tile([P, H], U8, name=f"w_sc{w}", align_bytes=64) for w in (W1, W2, W3)]
 
-        xa_w, xa_s = gathered("xa")
-        xb_w, xb_s = gathered("xb")
-        wd = [keep.tile([P, 2 * H], U8, name=f"wd{i}", align_bytes=64) for i in range(3)]
-        wsd = [keep.tile([P, H], U8, name=f"wsd{i}", align_bytes=64) for i in range(3)]
-
-        def deal_scales(engine, i):
-            engine.tensor_copy(
-                wsd[i][:].rearrange("p (t m) -> p t m", t=PACK), wsr[i][:].rearrange("p (m t) -> p t m", t=PACK)
+        def deal_scales(w):
+            nc.gpsimd.tensor_copy(
+                w_sc[w][:].rearrange("p (r m) -> p r m", r=SLOTS), raw_sc[w][:].rearrange("p (m r) -> p r m", r=SLOTS)
             )
 
-        def deal_words_scalar(i, raw):
+        def deal_words(w, raw):
             nc.scalar.copy(
-                wd[i][:].bitcast(U16).rearrange("p (t m) -> p t m", t=PACK),
-                raw[:].bitcast(U16).rearrange("p (m t) -> p t m", t=PACK),
+                w_wd[w][:].bitcast(U16).rearrange("p (r m) -> p r m", r=SLOTS),
+                raw[:].bitcast(U16).rearrange("p (m r) -> p r m", r=SLOTS),
             )
 
-        nc.vector.tensor_copy(xa_s[:], xs[:].indirect(l_offs[:]))
-        nc.vector.tensor_copy(xb_s[:], xs[:].indirect(l_two[:]))
-        deal_words_scalar(0, w1r)
-        deal_scales(nc.gpsimd, 0)
-        nc.vector.tensor_copy(xa_w[:], xw[:].indirect(l_offs[:]))
-        nc.vector.tensor_copy(xb_w[:], xw[:].indirect(l_two[:]))
-        g_y = keep.tile([P, PACK], F32, name="g_y")
-        nc.scalar.activation(g_y[:], gn_t[:], ACT.Copy, scale=-0.5)
-        g_ds = keep.tile([P, 1], F32, name="g_ds")
-        nc.scalar.activation(g_ds[:], gn_t[:, 0:1], ACT.Copy, scale=2.0)
-        deal_words_scalar(2, w3r)
-        deal_words_scalar(1, w2r)
-        deal_scales(nc.gpsimd, 2)
-        nsl = keep.tile([P, PACK], F32, name="nsl", tag="wsr2")
-        nc.gpsimd.tensor_scalar(nsl[:], sl_t[:], -1.0, 0.0, ALU.mult, ALU.add)
-        sbias = keep.tile([P, PACK], F32, name="sbias", tag="sbias", align_bytes=64)
-        nc.gpsimd.tensor_tensor(sbias[:], nsl[:], th_t[:], ALU.mult)
+        nc.vector.tensor_copy(offs_sc[:], x_sc[:].indirect(list_offs[:]))
+        nc.vector.tensor_copy(two_sc[:], x_sc[:].indirect(list_two[:]))
+        deal_words(W1, raw_w1)
+        deal_scales(W1)
+        nc.vector.tensor_copy(offs_wd[:], x_wd[:].indirect(list_offs[:]))
+        nc.vector.tensor_copy(two_wd[:], x_wd[:].indirect(list_two[:]))
 
-        def product(dst, i, t, codes, scales):
+        neg_half_gn = keep.tile([P, LAST], F32, name="neg_half_gn")
+        nc.scalar.activation(neg_half_gn[:], gn_sb[:, 1:SLOTS], ACT.Copy, scale=-0.5)
+        twice_gn = keep.tile([P, 1], F32, name="twice_gn")
+        nc.scalar.activation(twice_gn[:], gn_sb[:, 0:1], ACT.Copy, scale=2.0)
+        deal_words(W3, raw_w3)
+        deal_words(W2, raw_w2)
+        deal_scales(W3)
+        neg_sl = keep.tile([P, SLOTS], F32, name="neg_sl", tag=f"raw_sc{W3}")
+        nc.gpsimd.tensor_scalar(neg_sl[:], sl_sb[:], -1.0, 0.0, ALU.mult, ALU.add)
+        sg_bias = keep.tile([P, SLOTS], F32, name="sg_bias", tag="sg_bias", align_bytes=64)
+        nc.gpsimd.tensor_tensor(sg_bias[:], neg_sl[:], th_sb[:], ALU.mult)
+
+        def product(dst, w, r, codes, scales):
             nc.tensor.matmul_mx(
                 dst,
-                lhsT=wd[i][:, 2 * P * t : 2 * P * (t + 1)].bitcast(FP4X4),
-                lhsT_scale=wsd[i][:, P * t : P * (t + 1)],
+                lhsT=w_wd[w][:, 2 * P * r : 2 * P * (r + 1)].bitcast(FP4X4),
+                lhsT_scale=w_sc[w][:, P * r : P * (r + 1)],
                 rhs=codes.bitcast(FP8X4),
                 rhs_scale=scales,
                 start=True,
                 stop=True,
             )
 
-        y_ps = [psum.tile([P, S], F32, name=f"y_ps{t}", tag=f"bank{t}") for t in range(PACK)]
-        d_ps = [psum.tile([P, S], F32, name=f"d_ps{t}", tag=f"bank{4 + t}") for t in range(PACK)]
-        for t in range(PACK):
-            product(y_ps[t][:], 0, t, xa_w[:], xa_s[:])
-        for t in range(PACK):
-            product(d_ps[t][:], 2, t, xb_w[:], xb_s[:])
+        y_ps = [psum.tile([P, S], F32, name=f"y_ps{r}", tag=f"bank{r}") for r in range(SLOTS)]
+        d_ps = [psum.tile([P, S], F32, name=f"d_ps{r}", tag=f"bank{SLOTS + r}") for r in range(SLOTS)]
+        for r in range(SLOTS):
+            product(y_ps[r][:], W1, r, offs_wd[:], offs_sc[:])
+        for r in range(SLOTS):
+            product(d_ps[r][:], W3, r, two_wd[:], two_sc[:])
 
-        y = [keep.tile([P, WINDOW], F32, name=f"y{t}", tag=f"y{t}") for t in range(PACK)]
-        y2 = [keep.tile([P, S], F32, name=f"y2_{t}") for t in range(1, PACK)]
-        sm = [keep.tile([P, S], F32, name=f"sm{t}") for t in range(PACK)]
-        ea = [keep.tile([P, S], F32, name=f"ea{t}", tag=f"ea{t}") for t in range(PACK)]
-        top = [keep.tile([P, 1], F32, name=f"top{t}") for t in range(PACK)]
-        ebias = [keep.tile([P, 1], F32, name=f"ebias{t}") for t in range(PACK)]
-        for t in range(PACK):
-            nc.vector.tensor_scalar(y[t][:, 0:S], y_ps[t][:], 1.0, None, ALU.mult, ALU.max, accum_out=top[t][:])
-            nc.gpsimd.tensor_scalar(ebias[t][:], top[t][:], tau_t[:, t : t + 1], -1.0, ALU.mult, ALU.mult)
+        y = [keep.tile([P, WINDOW], F32, name=f"y{r}", tag=f"y{r}") for r in range(SLOTS)]
+        y_gn = [keep.tile([P, S], F32, name=f"y_gn{r}") for r in range(1, SLOTS)]
+        sm = [keep.tile([P, S], F32, name=f"sm{r}") for r in range(SLOTS)]
+        ea = [keep.tile([P, S], F32, name=f"ea{r}", tag=f"ea{r}") for r in range(SLOTS)]
+        top = [keep.tile([P, 1], F32, name=f"top{r}") for r in range(SLOTS)]
+        ea_bias = [keep.tile([P, 1], F32, name=f"ea_bias{r}") for r in range(SLOTS)]
+        for r in range(SLOTS):
+            nc.vector.tensor_scalar(y[r][:, 0:S], y_ps[r][:], 1.0, None, ALU.mult, ALU.max, accum_out=top[r][:])
+            nc.gpsimd.tensor_scalar(ea_bias[r][:], top[r][:], tau_sb[:, r : r + 1], -1.0, ALU.mult, ALU.mult)
             nc.scalar.activation(
-                ea[t][:], y[t][:].indirect(l_n1[:]), ACT.Exp, bias=ebias[t][:], scale=tau_t[:, t : t + 1]
+                ea[r][:], y[r][:].indirect(list_n1[:]), ACT.Exp, bias=ea_bias[r][:], scale=tau_sb[:, r : r + 1]
             )
-        nc.vector.scalar_tensor_tensor(sm[0][:], y_ps[0][:], g_ds[:], ea[0][:], ALU.mult, ALU.mult)
-        for t in range(1, PACK):
-            nc.gpsimd.tensor_scalar(y2[t - 1][:], y[t][:, 0:S], gn_t[:, t : t + 1], 2.0, ALU.mult, ALU.mult)
-            nc.gpsimd.tensor_tensor(sm[t][:], y2[t - 1][:], ea[t][:], ALU.mult)
+        nc.vector.scalar_tensor_tensor(sm[0][:], y_ps[0][:], twice_gn[:], ea[0][:], ALU.mult, ALU.mult)
+        for r in range(1, SLOTS):
+            nc.gpsimd.tensor_scalar(y_gn[r - 1][:], y[r][:, 0:S], gn_sb[:, r : r + 1], 2.0, ALU.mult, ALU.mult)
+            nc.gpsimd.tensor_tensor(sm[r][:], y_gn[r - 1][:], ea[r][:], ALU.mult)
 
-        ds = [keep.tile([P, WINDOW], F32, name=f"ds{t}") for t in range(PACK)]
-        zp = keep.tile([P, PACK, S], BF16, name="zp")
-        nc.vector.tensor_copy(ds[0][:].indirect(l_n2[:]), sm[0][:])
-        yneg = keep.tile([P, S], F32, name="yneg", tag=f"ea{PACK - 1}")
-        nc.gpsimd.tensor_scalar(yneg[:], y[0][:, 0:S], gn_t[:, 0:1], -0.5, ALU.mult, ALU.mult)
-        nc.gpsimd.tensor_tensor(zp[:, 0, :], ds[0][:, 0:S], yneg[:], ALU.add)
+        ds = [keep.tile([P, WINDOW], F32, name=f"ds{r}") for r in range(SLOTS)]
+        z = keep.tile([P, SLOTS, S], BF16, name="z")
+        nc.vector.tensor_copy(ds[0][:].indirect(list_n2[:]), sm[0][:])
+        neg_y0 = keep.tile([P, S], F32, name="neg_y0", tag=f"ea{LAST}")
+        nc.gpsimd.tensor_scalar(neg_y0[:], y[0][:, 0:S], gn_sb[:, 0:1], -0.5, ALU.mult, ALU.mult)
+        nc.gpsimd.tensor_tensor(z[:, 0, :], ds[0][:, 0:S], neg_y0[:], ALU.add)
 
-        d = [keep.tile([P, WINDOW], F32, name=f"d{t}") for t in range(PACK)]
-        dg = [keep.tile([P, S], F32, name=f"dg{t}") for t in range(PACK)]
-        e = keep.tile([P, PACK, S], F32, name="e")
-        for t in range(PACK):
-            nc.scalar.copy(d[t][:, 0:S], d_ps[t][:])
-            nc.scalar.activation(dg[t][:], d[t][:].indirect(l_n4[:]), ACT.Copy)
-            nc.gpsimd.tensor_tensor(e[:, t, :], dg[t][:], d[t][:, 0:S], ALU.subtract)
-        deal_scales(nc.gpsimd, 1)
-        sg = keep.tile([P, PACK, S], F32, name="sg", tag=f"y{PACK - 1}")
-        for t in range(PACK):
-            nc.scalar.activation(
-                sg[:, t, :], d[t][:].indirect(l_n3[:]), ACT.Sigmoid, bias=sbias[:, t : t + 1], scale=sl_t[:, t : t + 1]
-            )
+        d = [keep.tile([P, WINDOW], F32, name=f"d{r}") for r in range(SLOTS)]
+        d_n4 = [keep.tile([P, S], F32, name=f"d_n4_{r}") for r in range(SLOTS)]
+        diff = keep.tile([P, SLOTS, S], F32, name="diff")
+        for r in range(SLOTS):
+            nc.scalar.copy(d[r][:, 0:S], d_ps[r][:])
+            nc.scalar.activation(d_n4[r][:], d[r][:].indirect(list_n4[:]), ACT.Copy)
+            nc.gpsimd.tensor_tensor(diff[:, r, :], d_n4[r][:], d[r][:, 0:S], ALU.subtract)
+        deal_scales(W2)
+        sg = keep.tile([P, 2, SLOTS, S // 2], F32, name="sg", tag=f"y{LAST}")
+        for half in range(2):
+            for r in range(SLOTS):
+                nc.scalar.activation(
+                    sg[:, half, r, :],
+                    d[r][:].indirect(list_n3[:, half * LIST_COLS // 2 : (half + 1) * LIST_COLS // 2]),
+                    ACT.Sigmoid,
+                    bias=sg_bias[:, r : r + 1],
+                    scale=sl_sb[:, r : r + 1],
+                )
 
-        def make_z(t, cols):
+        def make_z(r, cols):
             nc.vector.scalar_tensor_tensor(
-                zp[:, t, cols], y_ps[t][:, cols], g_y[:, t : t + 1], ds[t][:, cols], ALU.mult, ALU.add
+                z[:, r, cols], y_ps[r][:, cols], neg_half_gn[:, r - 1 : r], ds[r][:, cols], ALU.mult, ALU.add
             )
 
-        for t in range(1, PACK):
-            nc.vector.tensor_copy(ds[t][:].indirect(l_n2[:]), sm[t][:])
-            if t > 1:
-                make_z(t - 1, slice(0, S))
+        for r in range(1, SLOTS):
+            nc.vector.tensor_copy(ds[r][:].indirect(list_n2[:]), sm[r][:])
+            if r > 1:
+                make_z(r - 1, slice(0, S))
 
-        chunks = [slice(c * CHUNK, (c + 1) * CHUNK) for c in range(NCHUNK)]
+        chunks = [slice(c * CHUNK, (c + 1) * CHUNK) for c in range(CHUNKS)]
+        final = CHUNKS - 1
 
-        def interleave(copy, dst, src):
+        def weave(copy, dst, src):
             copy(
-                dst.rearrange("p (c i t) -> p c t i", i=4, t=PACK),
-                src.rearrange("p t (c i) -> p c t i", i=4),
+                dst.rearrange("p (c i r) -> p c r i", i=4, r=SLOTS),
+                src.rearrange("p r (c i) -> p c r i", i=4),
             )
 
-        zi_first = keep.tile([P, 2, PACK * CHUNK], BF16, name="zi_first", align_bytes=64)
-        zi_rest = keep.tile([P, 2, PACK * CHUNK], BF16, name="zi_rest", tag="sbias", align_bytes=64)
-        zi = [zi_first[:, 0, :], zi_first[:, 1, :], zi_rest[:, 0, :], zi_rest[:, 1, :]]
-        oi = [keep.tile([P, PACK * CHUNK], BF16, name=f"oi{c}", align_bytes=64) for c in range(NCHUNK)]
-        zq_w = [keep.tile([P, CHUNK], U32, name=f"zq_w{c}", align_bytes=64) for c in range(NCHUNK)]
-        zq_s = [keep.tile([P, CHUNK], U8, name=f"zq_s{c}", align_bytes=64) for c in range(NCHUNK)]
-        oq_w = keep.tile([P, S], U32, name="oq_w", align_bytes=64)
-        oq_s = keep.tile([P, S], U8, name="oq_s", align_bytes=64)
-        hs = [keep.tile([P, PACK, CHUNK], F32, name=f"hs{c}") for c in range(NCHUNK)]
-        res = [keep.tile([P, PACK, CHUNK], F32, name=f"res{c}") for c in range(NCHUNK)]
-        h_ps = [psum.tile([P, PACK, CHUNK], F32, name=f"h_ps{c}", tag=f"bank{4 + c}") for c in range(NCHUNK)]
-        out_rows = out_0.rearrange("(p t) c -> p t c", t=PACK)
+        z_woven_vector = keep.tile([P, final, SLOTS * CHUNK], BF16, name="z_woven_vector", align_bytes=64)
+        z_woven_scalar = keep.tile([P, SLOTS * CHUNK], BF16, name="z_woven_scalar", tag="sg_bias", align_bytes=64)
+        z_woven = [z_woven_vector[:, c, :] for c in range(final)] + [z_woven_scalar[:]]
+        out_woven = [keep.tile([P, SLOTS * CHUNK], BF16, name=f"out_woven{c}", align_bytes=64) for c in range(CHUNKS)]
+        z_wd = [keep.tile([P, CHUNK], U32, name=f"z_wd{c}", align_bytes=64) for c in range(CHUNKS)]
+        z_sc = [keep.tile([P, CHUNK], U8, name=f"z_sc{c}", align_bytes=64) for c in range(CHUNKS)]
+        out_wd = keep.tile([P, S], U32, name="out_wd", align_bytes=64)
+        out_sc = keep.tile([P, S], U8, name="out_sc", align_bytes=64)
+        gated = [keep.tile([P, SLOTS, CHUNK], F32, name=f"gated{c}") for c in range(CHUNKS)]
+        result = [keep.tile([P, SLOTS, CHUNK], F32, name=f"result{c}") for c in range(CHUNKS)]
+        h_ps = [psum.tile([P, SLOTS, CHUNK], F32, name=f"h_ps{c}", tag=f"bank{SLOTS + c}") for c in range(CHUNKS)]
+        out_rows = out_0.rearrange("(p r) c -> p r c", r=SLOTS)
         out_words = out_1[0].rearrange("p c r -> p (c r)").bitcast(I32)
 
-        def second_product(c):
-            nc.vector.quantize_mx(zq_w[c][:].bitcast(FP8X4), zq_s[c][:], zi[c])
-            for t in range(PACK):
-                product(h_ps[c][:, t, :], 1, t, zq_w[c][:], zq_s[c][:])
+        def weave_z(copy, c):
+            weave(copy, z_woven[c], z[:, :, chunks[c]])
+
+        def make_h(c):
+            nc.vector.quantize_mx(z_wd[c][:].bitcast(FP8X4), z_sc[c][:], z_woven[c])
+            for r in range(SLOTS):
+                product(h_ps[c][:, r, :], W2, r, z_wd[c][:], z_sc[c][:])
 
         def gate(c):
-            nc.vector.tensor_tensor(hs[c][:], h_ps[c][:], sg[:, :, chunks[c]], ALU.mult)
+            nc.vector.tensor_tensor(gated[c][:], h_ps[c][:], sg[:, c // 2, :, chunks[c % 2]], ALU.mult)
 
         def combine(c):
-            nc.vector.tensor_tensor(res[c][:], hs[c][:], e[:, :, chunks[c]], ALU.max)
-            nc.sync.dma_start(out_rows[:, :, chunks[c]], res[c][:])
-            if c < NCHUNK - 1:
-                interleave(nc.scalar.copy, oi[c][:], res[c][:])
+            nc.vector.tensor_tensor(result[c][:], gated[c][:], diff[:, :, chunks[c]], ALU.max)
+            nc.sync.dma_start(out_rows[:, :, chunks[c]], result[c][:])
+            if c != final:
+                weave(nc.scalar.copy, out_woven[c][:], result[c][:])
 
-        def planes(c):
-            nc.vector.quantize_mx(oq_w[:, chunks[c]].bitcast(FP8X4), oq_s[:, chunks[c]], oi[c][:])
-            nc.sync.dma_start(out_words[:, chunks[c]], oq_w[:, chunks[c]].bitcast(I32))
+        def quantise_out(c):
+            nc.vector.quantize_mx(out_wd[:, chunks[c]].bitcast(FP8X4), out_sc[:, chunks[c]], out_woven[c][:])
+            nc.sync.dma_start(out_words[:, chunks[c]], out_wd[:, chunks[c]].bitcast(I32))
 
-        make_z(PACK - 1, chunks[0])
-        make_z(PACK - 1, chunks[1])
-        interleave(nc.vector.tensor_copy, zi[0], zp[:, :, chunks[0]])
-        make_z(PACK - 1, slice(2 * CHUNK, S))
-        second_product(0)
-        interleave(nc.vector.tensor_copy, zi[1], zp[:, :, chunks[1]])
-        for c in (2, 3):
-            interleave(nc.scalar.copy, zi[c], zp[:, :, chunks[c]])
-        second_product(1)
+        make_z(LAST, chunks[0])
+        make_z(LAST, chunks[1])
+        weave_z(nc.vector.tensor_copy, 0)
+        make_z(LAST, slice(2 * CHUNK, S))
+        make_h(0)
+        weave_z(nc.vector.tensor_copy, 1)
+        weave_z(nc.scalar.copy, final)
+        weave_z(nc.vector.tensor_copy, 2)
+        make_h(1)
+        make_h(2)
         gate(0)
-        second_product(2)
         gate(1)
         combine(0)
-        second_product(3)
-        gate(2)
         combine(1)
-        gate(3)
+        gate(2)
+        make_h(final)
+        gate(final)
         combine(2)
-        planes(0)
-        combine(3)
-        planes(1)
-        interleave(nc.vector.tensor_copy, oi[3][:], res[3][:])
-        planes(2)
-        planes(3)
-        for q in range(4):
+        quantise_out(0)
+        combine(final)
+        quantise_out(1)
+        weave(nc.vector.tensor_copy, out_woven[final][:], result[final][:])
+        quantise_out(2)
+        quantise_out(final)
+        for q in range(QUADRANTS):
             queue = nc.scalar if q % 2 == 0 else nc.sync
-            queue.dma_start(out_2[0, 4 * q : 4 * q + 4, :].bitcast(I32), oq_s[32 * q : 32 * q + 4, :].bitcast(I32))
+            queue.dma_start(
+                out_2[0, 4 * q : 4 * q + 4, :].bitcast(I32), out_sc[32 * q : 32 * q + 4, :].bitcast(I32)
+            )

from contextlib import ExitStack

import concourse.mybir as mybir

K, T, S, N, H = 512, 2048, 512, 512, 512
FLOPS = 2 * S * (K * H + H * N + K * N)

F32 = mybir.dt.float32
BF16 = mybir.dt.bfloat16
I32 = mybir.dt.int32
U32 = mybir.dt.uint32
U16 = mybir.dt.uint16
U8 = mybir.dt.uint8
FP8X4 = mybir.dt.float8_e4m3fn_x4
FP4X4 = mybir.dt.float4_e2m1fn_x4
ALU = mybir.AluOpType
ACT = mybir.ActivationFunctionType

P = 128
SLOTS = 4
LAST = SLOTS - 1
QUADRANTS = 4
LIST_COLS = S // 16
WINDOW = 2 * S
CHUNK = 128
CHUNKS = S // CHUNK
W1, W2, W3 = 0, 1, 2


def tile_picked_latemxbesd_none_po_kernel(
    tc, x_words, x_scales, w1_words, w1_scales, tau, gn, w2_words, w2_scales, w3_words, w3_scales,
    sl, th, offs, n1, n2, two, n3, n4, out_0, out_1, out_2,
):
    nc = tc.nc
    with ExitStack() as ctx:
        keep = ctx.enter_context(tc.tile_pool(name="keep", bufs=1))
        psum = ctx.enter_context(tc.psum_pool(name="psum", bufs=1))

        def load_list(src, name):
            tile = keep.tile([P, LIST_COLS], U16, name=name)
            nc.sync.dma_start(tile[:], src)
            return tile

        def load_scale_rows(queues, dst, src):
            for q in range(QUADRANTS):
                queues[q // 2].dma_start(
                    dst[32 * q : 32 * q + 4, :].bitcast(I32), src[0, 4 * q : 4 * q + 4, :].bitcast(I32)
                )

        def load_row_values(src, name):
            tile = keep.tile([P, SLOTS], F32, name=name)
            nc.gpsimd.dma_start(tile[:], src.rearrange("(p r) o -> p (r o)", r=SLOTS))
            return tile

        def load_weight_words(src, name):
            tile = keep.tile([P, 2 * H], U8, name=name)
            nc.sync.dma_start(tile[:].bitcast(I32), src[0].bitcast(I32))
            return tile

        x_sc = keep.tile([P, T], U8, name="x_sc")
        nc.vector.memset(x_sc[:].bitcast(I32), 0)
        raw_sc = [keep.tile([P, H], U8, name=f"raw_sc{w}", tag=f"raw_sc{w}") for w in (W1, W2, W3)]
        for w in (W1, W3, W2):
            nc.gpsimd.memset(raw_sc[w][:].bitcast(I32), 0)

        list_offs = load_list(offs, "list_offs")
        list_two = load_list(two, "list_two")
        load_scale_rows((nc.sync, nc.scalar), x_sc, x_scales)
        x_wd = keep.tile([P, T], U32, name="x_wd")
        nc.sync.dma_start(x_wd[:].bitcast(I32), x_words[0].rearrange("p c r -> p (c r)").bitcast(I32))
        raw_w1 = load_weight_words(w1_words, "raw_w1")
        load_scale_rows((nc.sync, nc.sync), raw_sc[W1], w1_scales)
        tau_sb = load_row_values(tau, "tau_sb")
        gn_sb = load_row_values(gn, "gn_sb")
        sl_sb = load_row_values(sl, "sl_sb")
        th_sb = load_row_values(th, "th_sb")
        list_n1 = load_list(n1, "list_n1")
        raw_w3 = load_weight_words(w3_words, "raw_w3")
        raw_w2 = load_weight_words(w2_words, "raw_w2")
        load_scale_rows((nc.sync, nc.sync), raw_sc[W3], w3_scales)
        list_n2 = load_list(n2, "list_n2")
        list_n4 = load_list(n4, "list_n4")
        load_scale_rows((nc.sync, nc.sync), raw_sc[W2], w2_scales)
        list_n3 = load_list(n3, "list_n3")

        offs_wd = keep.tile([P, S], U32, name="offs_wd", align_bytes=64)
        offs_sc = keep.tile([P, S], U8, name="offs_sc", align_bytes=64)
        two_wd = keep.tile([P, S], U32, name="two_wd", align_bytes=64)
        two_sc = keep.tile([P, S], U8, name="two_sc", align_bytes=64)
        w_wd = [keep.tile([P, 2 * H], U8, name=f"w_wd{w}", align_bytes=64) for w in (W1, W2, W3)]
        w_sc = [keep.tile([P, H], U8, name=f"w_sc{w}", align_bytes=64) for w in (W1, W2, W3)]

        def deal_scales(w):
            nc.gpsimd.tensor_copy(
                w_sc[w][:].rearrange("p (r m) -> p r m", r=SLOTS), raw_sc[w][:].rearrange("p (m r) -> p r m", r=SLOTS)
            )

        def deal_words(w, raw):
            nc.scalar.copy(
                w_wd[w][:].bitcast(U16).rearrange("p (r m) -> p r m", r=SLOTS),
                raw[:].bitcast(U16).rearrange("p (m r) -> p r m", r=SLOTS),
            )

        nc.vector.tensor_copy(offs_sc[:], x_sc[:].indirect(list_offs[:]))
        nc.vector.tensor_copy(two_sc[:], x_sc[:].indirect(list_two[:]))
        deal_words(W1, raw_w1)
        deal_scales(W1)
        nc.vector.tensor_copy(offs_wd[:], x_wd[:].indirect(list_offs[:]))
        nc.vector.tensor_copy(two_wd[:], x_wd[:].indirect(list_two[:]))

        neg_half_gn = keep.tile([P, LAST], F32, name="neg_half_gn")
        nc.scalar.activation(neg_half_gn[:], gn_sb[:, 1:SLOTS], ACT.Copy, scale=-0.5)
        twice_gn = keep.tile([P, 1], F32, name="twice_gn")
        nc.scalar.activation(twice_gn[:], gn_sb[:, 0:1], ACT.Copy, scale=2.0)
        deal_words(W3, raw_w3)
        deal_words(W2, raw_w2)
        deal_scales(W3)
        neg_sl = keep.tile([P, SLOTS], F32, name="neg_sl", tag=f"raw_sc{W3}")
        nc.gpsimd.tensor_scalar(neg_sl[:], sl_sb[:], -1.0, 0.0, ALU.mult, ALU.add)
        sg_bias = keep.tile([P, SLOTS], F32, name="sg_bias", tag="sg_bias", align_bytes=64)
        nc.gpsimd.tensor_tensor(sg_bias[:], neg_sl[:], th_sb[:], ALU.mult)

        def product(dst, w, r, codes, scales):
            nc.tensor.matmul_mx(
                dst,
                lhsT=w_wd[w][:, 2 * P * r : 2 * P * (r + 1)].bitcast(FP4X4),
                lhsT_scale=w_sc[w][:, P * r : P * (r + 1)],
                rhs=codes.bitcast(FP8X4),
                rhs_scale=scales,
                start=True,
                stop=True,
            )

        y_ps = [psum.tile([P, S], F32, name=f"y_ps{r}", tag=f"bank{r}") for r in range(SLOTS)]
        d_ps = [psum.tile([P, S], F32, name=f"d_ps{r}", tag=f"bank{SLOTS + r}") for r in range(SLOTS)]
        for r in range(SLOTS):
            product(y_ps[r][:], W1, r, offs_wd[:], offs_sc[:])
        for r in range(SLOTS):
            product(d_ps[r][:], W3, r, two_wd[:], two_sc[:])

        y = [keep.tile([P, WINDOW], F32, name=f"y{r}", tag=f"y{r}") for r in range(SLOTS)]
        y_gn = [keep.tile([P, S], F32, name=f"y_gn{r}") for r in range(1, SLOTS)]
        sm = [keep.tile([P, S], F32, name=f"sm{r}") for r in range(SLOTS)]
        ea = [keep.tile([P, S], F32, name=f"ea{r}", tag=f"ea{r}") for r in range(SLOTS)]
        top = [keep.tile([P, 1], F32, name=f"top{r}") for r in range(SLOTS)]
        ea_bias = [keep.tile([P, 1], F32, name=f"ea_bias{r}") for r in range(SLOTS)]
        for r in range(SLOTS):
            nc.vector.tensor_scalar(y[r][:, 0:S], y_ps[r][:], 1.0, None, ALU.mult, ALU.max, accum_out=top[r][:])
            nc.gpsimd.tensor_scalar(ea_bias[r][:], top[r][:], tau_sb[:, r : r + 1], -1.0, ALU.mult, ALU.mult)
            nc.scalar.activation(
                ea[r][:], y[r][:].indirect(list_n1[:]), ACT.Exp, bias=ea_bias[r][:], scale=tau_sb[:, r : r + 1]
            )
        nc.vector.scalar_tensor_tensor(sm[0][:], y_ps[0][:], twice_gn[:], ea[0][:], ALU.mult, ALU.mult)
        for r in range(1, SLOTS):
            nc.gpsimd.tensor_scalar(y_gn[r - 1][:], y[r][:, 0:S], gn_sb[:, r : r + 1], 2.0, ALU.mult, ALU.mult)
            nc.gpsimd.tensor_tensor(sm[r][:], y_gn[r - 1][:], ea[r][:], ALU.mult)

        ds = [keep.tile([P, WINDOW], F32, name=f"ds{r}") for r in range(SLOTS)]
        z = keep.tile([P, SLOTS, S], BF16, name="z")
        nc.vector.tensor_copy(ds[0][:].indirect(list_n2[:]), sm[0][:])
        neg_y0 = keep.tile([P, S], F32, name="neg_y0", tag=f"ea{LAST}")
        nc.gpsimd.tensor_scalar(neg_y0[:], y[0][:, 0:S], gn_sb[:, 0:1], -0.5, ALU.mult, ALU.mult)
        nc.gpsimd.tensor_tensor(z[:, 0, :], ds[0][:, 0:S], neg_y0[:], ALU.add)

        d = [keep.tile([P, WINDOW], F32, name=f"d{r}") for r in range(SLOTS)]
        d_n4 = [keep.tile([P, S], F32, name=f"d_n4_{r}") for r in range(SLOTS)]
        diff = keep.tile([P, SLOTS, S], F32, name="diff")
        for r in range(SLOTS):
            nc.scalar.copy(d[r][:, 0:S], d_ps[r][:])
            nc.scalar.activation(d_n4[r][:], d[r][:].indirect(list_n4[:]), ACT.Copy)
            nc.gpsimd.tensor_tensor(diff[:, r, :], d_n4[r][:], d[r][:, 0:S], ALU.subtract)
        deal_scales(W2)
        sg = keep.tile([P, 2, SLOTS, S // 2], F32, name="sg", tag=f"y{LAST}")
        for half in range(2):
            for r in range(SLOTS):
                nc.scalar.activation(
                    sg[:, half, r, :],
                    d[r][:].indirect(list_n3[:, half * LIST_COLS // 2 : (half + 1) * LIST_COLS // 2]),
                    ACT.Sigmoid,
                    bias=sg_bias[:, r : r + 1],
                    scale=sl_sb[:, r : r + 1],
                )

        def make_z(r, cols):
            nc.vector.scalar_tensor_tensor(
                z[:, r, cols], y_ps[r][:, cols], neg_half_gn[:, r - 1 : r], ds[r][:, cols], ALU.mult, ALU.add
            )

        for r in range(1, SLOTS):
            nc.vector.tensor_copy(ds[r][:].indirect(list_n2[:]), sm[r][:])
            if r > 1:
                make_z(r - 1, slice(0, S))

        chunks = [slice(c * CHUNK, (c + 1) * CHUNK) for c in range(CHUNKS)]
        final = CHUNKS - 1

        def weave(copy, dst, src):
            copy(
                dst.rearrange("p (c i r) -> p c r i", i=4, r=SLOTS),
                src.rearrange("p r (c i) -> p c r i", i=4),
            )

        z_woven_vector = keep.tile([P, final, SLOTS * CHUNK], BF16, name="z_woven_vector", align_bytes=64)
        z_woven_scalar = keep.tile([P, SLOTS * CHUNK], BF16, name="z_woven_scalar", tag="sg_bias", align_bytes=64)
        z_woven = [z_woven_vector[:, c, :] for c in range(final)] + [z_woven_scalar[:]]
        out_woven = [keep.tile([P, SLOTS * CHUNK], BF16, name=f"out_woven{c}", align_bytes=64) for c in range(CHUNKS)]
        z_wd = [keep.tile([P, CHUNK], U32, name=f"z_wd{c}", align_bytes=64) for c in range(CHUNKS)]
        z_sc = [keep.tile([P, CHUNK], U8, name=f"z_sc{c}", align_bytes=64) for c in range(CHUNKS)]
        out_wd = keep.tile([P, S], U32, name="out_wd", align_bytes=64)
        out_sc = keep.tile([P, S], U8, name="out_sc", align_bytes=64)
        gated = [keep.tile([P, SLOTS, CHUNK], F32, name=f"gated{c}") for c in range(CHUNKS)]
        result = [keep.tile([P, SLOTS, CHUNK], F32, name=f"result{c}") for c in range(CHUNKS)]
        h_ps = [psum.tile([P, SLOTS, CHUNK], F32, name=f"h_ps{c}", tag=f"bank{SLOTS + c}") for c in range(CHUNKS)]
        out_rows = out_0.rearrange("(p r) c -> p r c", r=SLOTS)
        out_words = out_1[0].rearrange("p c r -> p (c r)").bitcast(I32)

        def weave_z(copy, c):
            weave(copy, z_woven[c], z[:, :, chunks[c]])

        def make_h(c):
            nc.vector.quantize_mx(z_wd[c][:].bitcast(FP8X4), z_sc[c][:], z_woven[c])
            for r in range(SLOTS):
                product(h_ps[c][:, r, :], W2, r, z_wd[c][:], z_sc[c][:])

        def gate(c):
            nc.vector.tensor_tensor(gated[c][:], h_ps[c][:], sg[:, c // 2, :, chunks[c % 2]], ALU.mult)

        def combine(c):
            nc.vector.tensor_tensor(result[c][:], gated[c][:], diff[:, :, chunks[c]], ALU.max)
            nc.sync.dma_start(out_rows[:, :, chunks[c]], result[c][:])
            if c != final:
                weave(nc.scalar.copy, out_woven[c][:], result[c][:])

        def quantise_out(c):
            nc.vector.quantize_mx(out_wd[:, chunks[c]].bitcast(FP8X4), out_sc[:, chunks[c]], out_woven[c][:])
            nc.sync.dma_start(out_words[:, chunks[c]], out_wd[:, chunks[c]].bitcast(I32))

        make_z(LAST, chunks[0])
        make_z(LAST, chunks[1])
        weave_z(nc.vector.tensor_copy, 0)
        make_z(LAST, slice(2 * CHUNK, S))
        make_h(0)
        weave_z(nc.vector.tensor_copy, 1)
        weave_z(nc.scalar.copy, final)
        weave_z(nc.vector.tensor_copy, 2)
        make_h(1)
        make_h(2)
        gate(0)
        gate(1)
        combine(0)
        combine(1)
        gate(2)
        make_h(final)
        gate(final)
        combine(2)
        quantise_out(0)
        combine(final)
        quantise_out(1)
        weave(nc.vector.tensor_copy, out_woven[final][:], result[final][:])
        quantise_out(2)
        quantise_out(final)
        for q in range(QUADRANTS):
            queue = nc.scalar if q % 2 == 0 else nc.sync
            queue.dma_start(
                out_2[0, 4 * q : 4 * q + 4, :].bitcast(I32), out_sc[32 * q : 32 * q + 4, :].bitcast(I32)
            )
